import numpy as np
import ml_dtypes


def mxq(x, axis, fmt="e4m3"):
    dtype, down = {"e4m3": (ml_dtypes.float8_e4m3fn, 7), "e5m2": (ml_dtypes.float8_e5m2, 14)}[fmt]
    v = np.moveaxis(np.asarray(x, np.float32).astype(ml_dtypes.bfloat16).astype(np.float64), axis, -1)
    blocks = v.reshape(v.shape[:-1] + (-1, 32))
    amax = np.abs(blocks).max(-1, keepdims=True)
    byte = np.maximum(np.where(amax > 0, np.frexp(amax)[1] - 1 + 127, 0) - down, 1)
    scale = np.exp2(byte - 127.0)
    codes = (blocks / scale).astype(np.float32).astype(dtype).astype(np.float64)
    return np.moveaxis((codes * scale).reshape(v.shape), -1, axis)


WIDE = False


def mx_kscale(k):
    if not WIDE:
        return np.ones(k)
    levels = np.array([30, -30])
    if k % 512:
        return np.exp2(np.random.permutation(np.resize(levels, k // 32))).repeat(32)
    a = np.empty((k // 512, 16))
    for p in range(k // 512):
        a[p, :8] = np.random.permutation(np.resize(levels, 8))
        for g in range(8):
            far = levels[np.abs(levels - a[p, g]) >= 10]
            a[p, g + 8] = far[np.random.randint(len(far))]
    return np.exp2(a.ravel()).repeat(32)


def f64(x):
    return np.asarray(x).astype(np.float64)


def striped(idx):
    return np.tile(np.asarray(idx).reshape(-1, 16).T, (8, 1)).astype(np.uint16)


def unstriped(offs):
    return offs[:16].T.reshape(-1).astype(np.int64)


def striped8(idx):
    return np.asarray(idx).reshape(8, -1, 16).transpose(0, 2, 1).reshape(128, -1).astype(np.uint16)


def unstriped8(offs):
    return offs.reshape(8, 16, -1).transpose(0, 2, 1).reshape(8, -1).astype(np.int64)


def pick8(x, idx, run):
    r = np.arange(len(x))
    return x[r[:, None], idx[r % (8 * run) // run]]


E2M1 = np.array([0.0, 0.5, 1.0, 1.5, 2.0, 3.0, 4.0, 6.0, -0.0, -0.5, -1.0, -1.5, -2.0, -3.0, -4.0, -6.0])


def pack_weight(w, fmt):
    k, n = w.shape
    w = f64(np.asarray(w, np.float32).astype(ml_dtypes.bfloat16)).reshape(k // 32, 32, n)
    amax = np.abs(w).max(1)
    if fmt == "e4m3":
        byte = np.frexp(amax)[1] - 1 + 127 - 7
    else:
        mant, ex = np.frexp(amax / 6.0)
        byte = np.where(mant > 0.5, ex, ex - 1) + 127
    byte = np.clip(np.where(amax > 0, byte, 1), 1, 254)
    scaled = (w * np.exp2(127.0 - byte)[:, None, :]).reshape(k, n).astype(np.float32)
    by_word = np.ascontiguousarray(scaled.reshape(k // 512, 128, 4, n).transpose(0, 1, 3, 2))
    if fmt == "e4m3":
        words = by_word.astype(ml_dtypes.float8_e4m3fn).view(np.uint8)
    else:
        c = by_word.astype(ml_dtypes.float4_e2m1fn).view(np.uint8) & 0xF
        words = (c[..., 0::2] | (c[..., 1::2] << 4)).reshape(k // 512, 128, 2 * n)
    return np.ascontiguousarray(words), np.ascontiguousarray(byte.astype(np.uint8).reshape(k // 512, 16, n))


def unpack_weight(words, scales, fmt):
    g, _, n = scales.shape
    words = np.ascontiguousarray(words).reshape(g, 128, n, -1)
    if fmt == "e4m3":
        vals = words.view(ml_dtypes.float8_e4m3fn).astype(np.float64)
    else:
        nib = np.empty((g, 128, n, 4), np.uint8)
        nib[..., 0::2] = words & 0xF
        nib[..., 1::2] = words >> 4
        vals = E2M1[nib]
    vals = vals * np.repeat(np.exp2(scales.astype(np.float64) - 127.0), 8, axis=1)[..., None]
    return vals.transpose(0, 1, 3, 2).reshape(g * 512, n)


K, J, N, R, T, V = 512, 512, 256, 256, 1024, 1024


def setup_inputs():
    n = np.random.standard_normal
    idx = np.stack([np.random.permutation(T)[:J] for _ in range(8)])
    idx2 = np.random.permutation(V)[:J]
    fj = mx_kscale(J)
    fk = mx_kscale(K)
    drp = pack_weight(n((K, R)) * 1 / np.sqrt(K) / fk[:, None], "e4m3")
    return {
        "xf": (n((K, T))).astype(np.float32),
        "ra": (np.random.uniform(0.5, 1.5, (1, J)) * fj).astype(np.float32),
        "gt": (n((N, V)) * np.exp(0.5 * n((1, V)))).astype(np.float32),
        "rb": (np.random.uniform(0.5, 1.5, (1, J)) / fj).astype(np.float32),
        "cp": (np.random.uniform(0.4, 1.2, (N, 1))).astype(np.float32),
        "fkr": (np.random.uniform(0.5, 1.5, (1, K)) * fk).astype(np.float32),
        "dr_words": drp[0],
        "dr_scales": drp[1],
        "old": (12.0 * n((R, N))).astype(np.float32),
        "offs": striped8(idx),
        "offs2": striped(idx2),
    }


def reference(xf, ra, gt, rb, cp, fkr, dr_words, dr_scales, old, offs, offs2):
    idx = unstriped8(offs)
    idx2 = unstriped(offs2)
    dru = unpack_weight(dr_words, dr_scales, "e4m3")
    us = pick8(f64(xf), idx, 64) * f64(ra)
    ut = us.T
    uj = ut * f64(fkr)
    gs = np.minimum(f64(gt)[:, idx2], f64(cp)) * f64(rb)
    gj = gs.T
    ujq = mxq(uj, 0, "e4m3")
    gjq = mxq(gj, 0, "e5m2")
    w = ujq.T @ gjq
    wq = mxq(w, 0, "e5m2")
    v2 = dru.T @ wq
    y = 0.05 * np.maximum(v2, f64(old))
    return y

@@ -1,0 +1,167 @@
+from contextlib import ExitStack
+
+import concourse.mybir as mybir
+from concourse.masks import make_identity
+
+K, J, N, R, T, V = 512, 512, 256, 256, 1024, 1024
+FLOPS = 2 * J * K * N + 2 * K * R * N
+
+F32 = mybir.dt.float32
+BF16 = mybir.dt.bfloat16
+I32 = mybir.dt.int32
+U32 = mybir.dt.uint32
+U16 = mybir.dt.uint16
+U8 = mybir.dt.uint8
+E4M3 = mybir.dt.float8_e4m3fn_x4
+E5M2 = mybir.dt.float8_e5m2_x4
+ALU = mybir.AluOpType
+COPY = mybir.ActivationFunctionType.Copy
+
+P = 128
+PACK = 4
+KEEP = 0.05
+
+
+def tile_list_directions_headpicks_bounded_larger_kernel(
+    tc, xf, ra, gt, rb, cp, fkr, dr_words, dr_scales, old, offs, offs2, out
+):
+    nc = tc.nc
+    with ExitStack() as ctx:
+        lists = ctx.enter_context(tc.tile_pool(name="lists", bufs=1))
+        held = ctx.enter_context(tc.tile_pool(name="held", bufs=1))
+        psum = ctx.enter_context(tc.psum_pool(name="psum", bufs=1))
+        turn = ctx.enter_context(tc.psum_pool(name="turn", bufs=2))
+
+        x_list = lists.tile([P, J // 16], U16, name="x_list")
+        g_list = lists.tile([P, J // 16], U16, name="g_list")
+        x_rows = [held.tile([P, T], F32, name=f"x_rows{i}") for i in range(PACK)]
+        g_rows = [held.tile([P, V], F32, name=f"g_rows{h}") for h in range(2)]
+        ra_col = held.tile([P, PACK], F32, name="ra_col")
+        rb_col = held.tile([P, PACK], F32, name="rb_col")
+        fk_col = held.tile([P, PACK], F32, name="fk_col")
+        cp_col = held.tile([P, 2, 8], F32, name="cp_col")
+        dr_codes = held.tile([P, R], U32, name="dr_codes", align_bytes=64)
+        dr_plane = held.tile([P, R], U8, name="dr_plane", align_bytes=64)
+        old_rows = held.tile([P, 2, N], F32, name="old_rows")
+        old_kept = held.tile([P, 2, N], F32, name="old_kept")
+        ident = held.tile([P, P], F32, name="ident")
+
+        x_planes = xf.rearrange("(p i) t -> i p t", i=PACK)
+        g_halves = gt.rearrange("(h p) v -> h p v", h=2)
+
+        make_identity(nc, ident[:])
+        nc.gpsimd.memset(dr_plane[:].bitcast(I32), 0)
+
+        nc.sync.dma_start(rb_col[:], rb.rearrange("o (p a) -> p (o a)", a=PACK))
+        nc.sync.dma_start(g_rows[0][:], g_halves[0])
+        nc.sync.dma_start(g_list[:], offs2)
+        with nc.allow_non_contiguous_dma(reason="one bound a partition and half"):
+            nc.sync.dma_start(cp_col[:, :, 0:1], cp.rearrange("(h p) o -> p h o", h=2))
+        nc.sync.dma_start(ra_col[:], ra.rearrange("o (p a) -> p (o a)", a=PACK))
+        nc.sync.dma_start(fk_col[:], fkr.rearrange("o (p a) -> p (o a)", a=PACK))
+        nc.sync.dma_start(x_list[:], offs)
+        nc.sync.dma_start(x_rows[0][:], x_planes[0])
+        nc.sync.dma_start(x_rows[1][:], x_planes[1])
+        nc.sync.dma_start(x_rows[2][:], x_planes[2])
+        nc.sync.dma_start(x_rows[3][:], x_planes[3])
+        nc.sync.dma_start(g_rows[1][:], g_halves[1])
+        nc.sync.dma_start(dr_codes[:].bitcast(I32), dr_words[0].rearrange("p n t -> p (n t)").bitcast(I32))
+        for q in range(4):
+            nc.sync.dma_start(
+                dr_plane[32 * q : 32 * q + 4, :].bitcast(I32), dr_scales[0, 4 * q : 4 * q + 4, :].bitcast(I32)
+            )
+        nc.sync.dma_start(old_rows[:], old.rearrange("(h p) n -> p h n", h=2))
+
+        def spread(col, name):
+            bank = psum.tile([P, PACK, P], F32, name=name)
+            for a in range(PACK):
+                nc.tensor.transpose(bank[:, a, :], col[:, a : a + 1].to_broadcast([P, P]), ident[:])
+            return bank[:].rearrange("p a m -> p m a")
+
+        rb_all = spread(rb_col, "rb_all")
+        ra_all = spread(ra_col, "ra_all")
+
+        def operand(name, rows, offsets, scalar, op0, weights, on_vector, evac, fmt):
+            picked = held.tile([P, J], F32, name=name + "_picked")
+            rounded = held.tile([P, J], BF16, name=name + "_rounded", align_bytes=64)
+            parts = [(a, b) for a, b in ((0, on_vector), (on_vector, J)) if b > a]
+            for a, b in parts:
+                window = rows[:].indirect(offsets[:, a // 16 : b // 16])
+                if b <= on_vector:
+                    nc.vector.tensor_copy(picked[:, a:b], window)
+                else:
+                    nc.scalar.activation(picked[:, a:b], window, COPY)
+            for a, b in parts:
+                nc.vector.scalar_tensor_tensor(
+                    rounded[:, a:b].rearrange("p (m a) -> p m a", a=PACK),
+                    picked[:, a:b].rearrange("p (m a) -> p m a", a=PACK),
+                    scalar,
+                    weights[:, a // PACK : b // PACK, :],
+                    op0,
+                    ALU.mult,
+                )
+            words = rounded[:].bitcast(F32)
+            turned = turn.tile([P, 2, P], F32, name="turned")
+            for u in range(2):
+                nc.tensor.transpose(turned[:, u, :], words[:, u::2], ident[:])
+            grouped = held.tile([P, J], BF16, name=name + "_grouped", align_bytes=64)
+            evac(grouped[:].bitcast(F32).rearrange("p (c u) -> p c u", u=2), turned[:].rearrange("p u c -> p c u"))
+            codes = held.tile([P, P], U32, name=name + "_codes", align_bytes=64)
+            plane = held.tile([P, P], U8, name=name + "_plane", align_bytes=64)
+            nc.vector.quantize_mx(codes[:].bitcast(fmt), plane[:], grouped[:])
+            return codes, plane
+
+        on_s, on_v = nc.scalar.copy, nc.vector.tensor_copy
+
+        def g_operand(h, on_vector, evac):
+            return operand(f"g{h}", g_rows[h], g_list, cp_col[:, h, 0:1], ALU.min, rb_all, on_vector, evac, E5M2)
+
+        def x_operand(i, on_vector, evac):
+            return operand(f"x{i}", x_rows[i], x_list, fk_col[:, i : i + 1], ALU.mult, ra_all, on_vector, evac, E4M3)
+
+        def first_product(bank, i, x_op, g_op):
+            nc.tensor.matmul_mx(
+                bank[:, i, :],
+                lhsT=x_op[0][:].bitcast(E4M3),
+                lhsT_scale=x_op[1][:],
+                rhs=g_op[0][:].bitcast(E5M2),
+                rhs_scale=g_op[1][:],
+                start=True,
+                stop=True,
+            )
+
+        def finish(h, bank, evac):
+            w_grouped = held.tile([P, K], BF16, name=f"w_grouped{h}", align_bytes=64)
+            evac(w_grouped[:].rearrange("p (n i) -> p n i", i=PACK), bank[:].rearrange("p i n -> p n i"))
+            w_codes = held.tile([P, P], U32, name=f"w_codes{h}", align_bytes=64)
+            w_plane = held.tile([P, P], U8, name=f"w_plane{h}", align_bytes=64)
+            nc.vector.quantize_mx(w_codes[:].bitcast(E5M2), w_plane[:], w_grouped[:])
+            v2 = psum.tile([P, 2, P], F32, name=f"v2_{h}")
+            for rh in range(2):
+                nc.tensor.matmul_mx(
+                    v2[:, rh, :],
+                    lhsT=dr_codes[:, rh * P : (rh + 1) * P].bitcast(E4M3),
+                    lhsT_scale=dr_plane[:, rh * P : (rh + 1) * P],
+                    rhs=w_codes[:].bitcast(E5M2),
+                    rhs_scale=w_plane[:],
+                    start=True,
+                    stop=True,
+                )
+            result = held.tile([P, 2, P], F32, name=f"result{h}")
+            nc.vector.scalar_tensor_tensor(
+                result[:], v2[:], KEEP, old_kept[:, :, h * P : (h + 1) * P], ALU.mult, ALU.max
+            )
+            nc.sync.dma_start(out.rearrange("(h p) n -> p h n", h=2)[:, :, h * P : (h + 1) * P], result[:])
+
+        w_banks = [psum.tile([P, PACK, P], F32, name=f"w_bank{h}") for h in range(2)]
+        g0 = g_operand(0, 256, on_s)
+        x_ops = []
+        for i, (on_vector, evac) in enumerate(((0, on_v), (0, on_v), (0, on_s), (256, on_s))):
+            x_ops.append(x_operand(i, on_vector, evac))
+            first_product(w_banks[0], i, x_ops[i], g0)
+        g1 = g_operand(1, 192, on_s)
+        nc.scalar.mul(old_kept[:], old_rows[:], KEEP)
+        finish(0, w_banks[0], on_s)
+        for i in range(PACK):
+            first_product(w_banks[1], i, x_ops[i], g1)
+        finish(1, w_banks[1], on_s)

@@ -30,7 +30,7 @@ def tile_list_directions_headpicks_bounded_larger_kernel(
         lists = ctx.enter_context(tc.tile_pool(name="lists", bufs=1))
         held = ctx.enter_context(tc.tile_pool(name="held", bufs=1))
         psum = ctx.enter_context(tc.psum_pool(name="psum", bufs=1))
-        turn = ctx.enter_context(tc.psum_pool(name="turn", bufs=2))
+        turn = ctx.enter_context(tc.psum_pool(name="turn", bufs=4))
 
         x_list = lists.tile([P, J // 16], U16, name="x_list")
         g_list = lists.tile([P, J // 16], U16, name="g_list")
@@ -43,7 +43,6 @@ def tile_list_directions_headpicks_bounded_larger_kernel(
         dr_codes = held.tile([P, R], U32, name="dr_codes", align_bytes=64)
         dr_plane = held.tile([P, R], U8, name="dr_plane", align_bytes=64)
         old_rows = held.tile([P, 2, N], F32, name="old_rows")
-        old_kept = held.tile([P, 2, N], F32, name="old_kept")
         ident = held.tile([P, P], F32, name="ident")
 
         x_planes = xf.rearrange("(p i) t -> i p t", i=PACK)
@@ -52,11 +51,15 @@ def tile_list_directions_headpicks_bounded_larger_kernel(
         make_identity(nc, ident[:])
         nc.gpsimd.memset(dr_plane[:].bitcast(I32), 0)
 
+        warm = held.tile([P, 2], F32, name="warm")
+        nc.vector.memset(warm[:, 0:1], 0.0)
+        nc.scalar.activation(warm[:, 1:2], warm[:, 0:1], COPY)
         nc.sync.dma_start(rb_col[:], rb.rearrange("o (p a) -> p (o a)", a=PACK))
         nc.sync.dma_start(g_rows[0][:], g_halves[0])
         nc.sync.dma_start(g_list[:], offs2)
         with nc.allow_non_contiguous_dma(reason="one bound a partition and half"):
             nc.sync.dma_start(cp_col[:, :, 0:1], cp.rearrange("(h p) o -> p h o", h=2))
+        nc.sync.dma_start(g_rows[1][:], g_halves[1])
         nc.sync.dma_start(ra_col[:], ra.rearrange("o (p a) -> p (o a)", a=PACK))
         nc.sync.dma_start(fk_col[:], fkr.rearrange("o (p a) -> p (o a)", a=PACK))
         nc.sync.dma_start(x_list[:], offs)
@@ -64,7 +67,6 @@ def tile_list_directions_headpicks_bounded_larger_kernel(
         nc.sync.dma_start(x_rows[1][:], x_planes[1])
         nc.sync.dma_start(x_rows[2][:], x_planes[2])
         nc.sync.dma_start(x_rows[3][:], x_planes[3])
-        nc.sync.dma_start(g_rows[1][:], g_halves[1])
         nc.sync.dma_start(dr_codes[:].bitcast(I32), dr_words[0].rearrange("p n t -> p (n t)").bitcast(I32))
         for q in range(4):
             nc.sync.dma_start(
@@ -81,22 +83,30 @@ def tile_list_directions_headpicks_bounded_larger_kernel(
         rb_all = spread(rb_col, "rb_all")
         ra_all = spread(ra_col, "ra_all")
 
-        def operand(name, rows, offsets, scalar, op0, weights, on_vector, evac, fmt):
-            picked = held.tile([P, J], F32, name=name + "_picked")
-            rounded = held.tile([P, J], BF16, name=name + "_rounded", align_bytes=64)
-            parts = [(a, b) for a, b in ((0, on_vector), (on_vector, J)) if b > a]
-            for a, b in parts:
-                window = rows[:].indirect(offsets[:, a // 16 : b // 16])
-                if b <= on_vector:
-                    nc.vector.tensor_copy(picked[:, a:b], window)
-                else:
-                    nc.scalar.activation(picked[:, a:b], window, COPY)
-            for a, b in parts:
+        def on_scalar(picked, window):
+            nc.scalar.activation(picked, window, COPY)
+
+        on_vector = nc.vector.tensor_copy
+        sources = [(g_rows[h], g_list, cp_col[:, h, 0:1], ALU.min, rb_all, E5M2) for h in range(2)]
+        sources += [(x_rows[i], x_list, fk_col[:, i : i + 1], ALU.mult, ra_all, E4M3) for i in range(PACK)]
+        shared = [[(0, 256, on_vector), (256, J, on_scalar)]]
+        whole = [[(0, J, on_scalar)]]
+        halves = [[(0, 256, on_scalar)], [(256, J, on_scalar)]]
+        pieces = [shared, whole, shared, whole, whole, halves]
+
+        def pick_weigh_turn(n):
+            rows, offsets, scalar, op0, weights, fmt = sources[n]
+            rounded = held.tile([P, J], BF16, name=f"rounded{n}", tag=f"rounded{n}", align_bytes=64)
+            for m, gathers in enumerate(pieces[n]):
+                first, last = gathers[0][0], gathers[-1][1]
+                picked = held.tile([P, last - first], F32, name=f"picked{n}_{m}", tag=f"slot{n}_{m}", align_bytes=64)
+                for a, b, gather in gathers:
+                    gather(picked[:, a - first : b - first], rows[:].indirect(offsets[:, a // 16 : b // 16]))
                 nc.vector.scalar_tensor_tensor(
-                    rounded[:, a:b].rearrange("p (m a) -> p m a", a=PACK),
-                    picked[:, a:b].rearrange("p (m a) -> p m a", a=PACK),
+                    rounded[:, first:last].rearrange("p (m a) -> p m a", a=PACK),
+                    picked[:].rearrange("p (m a) -> p m a", a=PACK),
                     scalar,
-                    weights[:, a // PACK : b // PACK, :],
+                    weights[:, first // PACK : last // PACK, :],
                     op0,
                     ALU.mult,
                 )
@@ -104,64 +114,63 @@ def tile_list_directions_headpicks_bounded_larger_kernel(
             turned = turn.tile([P, 2, P], F32, name="turned")
             for u in range(2):
                 nc.tensor.transpose(turned[:, u, :], words[:, u::2], ident[:])
-            grouped = held.tile([P, J], BF16, name=name + "_grouped", align_bytes=64)
-            evac(grouped[:].bitcast(F32).rearrange("p (c u) -> p c u", u=2), turned[:].rearrange("p u c -> p c u"))
-            codes = held.tile([P, P], U32, name=name + "_codes", align_bytes=64)
-            plane = held.tile([P, P], U8, name=name + "_plane", align_bytes=64)
-            nc.vector.quantize_mx(codes[:].bitcast(fmt), plane[:], grouped[:])
+            return turned
+
+        def quantise(n, turned, tag, empty):
+            grouped = held.tile([P, J], BF16, name=f"grouped{n}", tag=tag, align_bytes=64)
+            empty(
+                grouped[:].bitcast(F32).rearrange("p (c u) -> p c u", u=2), turned[:].rearrange("p u c -> p c u")
+            )
+            codes = held.tile([P, P], U32, name=f"codes{n}", align_bytes=64)
+            plane = held.tile([P, P], U8, name=f"plane{n}", align_bytes=64)
+            nc.vector.quantize_mx(codes[:].bitcast(sources[n][5]), plane[:], grouped[:])
             return codes, plane
 
-        on_s, on_v = nc.scalar.copy, nc.vector.tensor_copy
-
-        def g_operand(h, on_vector, evac):
-            return operand(f"g{h}", g_rows[h], g_list, cp_col[:, h, 0:1], ALU.min, rb_all, on_vector, evac, E5M2)
-
-        def x_operand(i, on_vector, evac):
-            return operand(f"x{i}", x_rows[i], x_list, fk_col[:, i : i + 1], ALU.mult, ra_all, on_vector, evac, E4M3)
-
-        def first_product(bank, i, x_op, g_op):
-            nc.tensor.matmul_mx(
-                bank[:, i, :],
-                lhsT=x_op[0][:].bitcast(E4M3),
-                lhsT_scale=x_op[1][:],
-                rhs=g_op[0][:].bitcast(E5M2),
-                rhs_scale=g_op[1][:],
-                start=True,
-                stop=True,
-            )
-
-        def finish(h, bank, evac):
-            w_grouped = held.tile([P, K], BF16, name=f"w_grouped{h}", align_bytes=64)
-            evac(w_grouped[:].rearrange("p (n i) -> p n i", i=PACK), bank[:].rearrange("p i n -> p n i"))
-            w_codes = held.tile([P, P], U32, name=f"w_codes{h}", align_bytes=64)
-            w_plane = held.tile([P, P], U8, name=f"w_plane{h}", align_bytes=64)
-            nc.vector.quantize_mx(w_codes[:].bitcast(E5M2), w_plane[:], w_grouped[:])
-            v2 = psum.tile([P, 2, P], F32, name=f"v2_{h}")
-            for rh in range(2):
+        w_banks = [psum.tile([P, PACK, P], F32, name=f"w_bank{h}") for h in range(2)]
+        turned = [pick_weigh_turn(0), pick_weigh_turn(1)]
+        operands = [quantise(0, turned[0], "grouped0", nc.vector.tensor_copy)]
+        turned.append(pick_weigh_turn(2))
+        operands.append(quantise(1, turned[1], "grouped1", nc.vector.tensor_copy))
+        turned += [pick_weigh_turn(n) for n in range(3, 6)]
+        for n, tag in zip(range(2, 6), ("slot4_0", "slot5_0", "slot5_1", "grouped5")):
+            operands.append(quantise(n, turned[n], tag, nc.scalar.copy))
+            for h in range(2):
                 nc.tensor.matmul_mx(
-                    v2[:, rh, :],
-                    lhsT=dr_codes[:, rh * P : (rh + 1) * P].bitcast(E4M3),
-                    lhsT_scale=dr_plane[:, rh * P : (rh + 1) * P],
-                    rhs=w_codes[:].bitcast(E5M2),
-                    rhs_scale=w_plane[:],
+                    w_banks[h][:, n - 2, :],
+                    lhsT=operands[n][0][:].bitcast(E4M3),
+                    lhsT_scale=operands[n][1][:],
+                    rhs=operands[h][0][:].bitcast(E5M2),
+                    rhs_scale=operands[h][1][:],
                     start=True,
                     stop=True,
                 )
-            result = held.tile([P, 2, P], F32, name=f"result{h}")
-            nc.vector.scalar_tensor_tensor(
-                result[:], v2[:], KEEP, old_kept[:, :, h * P : (h + 1) * P], ALU.mult, ALU.max
-            )
-            nc.sync.dma_start(out.rearrange("(h p) n -> p h n", h=2)[:, :, h * P : (h + 1) * P], result[:])
-
-        w_banks = [psum.tile([P, PACK, P], F32, name=f"w_bank{h}") for h in range(2)]
-        g0 = g_operand(0, 256, on_s)
-        x_ops = []
-        for i, (on_vector, evac) in enumerate(((0, on_v), (0, on_v), (0, on_s), (256, on_s))):
-            x_ops.append(x_operand(i, on_vector, evac))
-            first_product(w_banks[0], i, x_ops[i], g0)
-        g1 = g_operand(1, 192, on_s)
+        old_kept = held.tile([P, 2, N], F32, name="old_kept", tag="rounded5", align_bytes=64)
         nc.scalar.mul(old_kept[:], old_rows[:], KEEP)
-        finish(0, w_banks[0], on_s)
-        for i in range(PACK):
-            first_product(w_banks[1], i, x_ops[i], g1)
-        finish(1, w_banks[1], on_s)
+
+        w_ops = []
+        w_grouped = [held.tile([P, K], BF16, name=f"w_grouped{h}", align_bytes=64) for h in range(2)]
+        for h, evac in enumerate((nc.scalar.copy, nc.vector.tensor_copy)):
+            evac(w_grouped[h][:].rearrange("p (n i) -> p n i", i=PACK), w_banks[h][:].rearrange("p i n -> p n i"))
+        for h in range(2):
+            w_codes = held.tile([P, P], U32, name=f"w_codes{h}", align_bytes=64)
+            w_plane = held.tile([P, P], U8, name=f"w_plane{h}", align_bytes=64)
+            nc.vector.quantize_mx(w_codes[:].bitcast(E5M2), w_plane[:], w_grouped[h][:])
+            w_ops.append((w_codes, w_plane))
+        out_halves = out.rearrange("(h p) n -> h p n", h=2)
+        for rh in range(2):
+            v2 = psum.tile([P, 2, P], F32, name=f"v2_{rh}", tag=("rb_all", "ra_all")[rh])
+            for h in range(2):
+                nc.tensor.matmul_mx(
+                    v2[:, h, :],
+                    lhsT=dr_codes[:, rh * P : (rh + 1) * P].bitcast(E4M3),
+                    lhsT_scale=dr_plane[:, rh * P : (rh + 1) * P],
+                    rhs=w_ops[h][0][:].bitcast(E5M2),
+                    rhs_scale=w_ops[h][1][:],
+                    start=True,
+                    stop=True,
+                )
+            result = held.tile([P, N], F32, name=f"result{rh}")
+            nc.vector.scalar_tensor_tensor(
+                result[:], v2[:].rearrange("p h n -> p (h n)"), KEEP, old_kept[:, rh, :], ALU.mult, ALU.max
+            )
+            nc.sync.dma_start(out_halves[rh], result[:])

@@ -54,14 +54,14 @@ def tile_list_directions_headpicks_bounded_larger_kernel(
         warm = held.tile([P, 2], F32, name="warm")
         nc.vector.memset(warm[:, 0:1], 0.0)
         nc.scalar.activation(warm[:, 1:2], warm[:, 0:1], COPY)
-        nc.sync.dma_start(rb_col[:], rb.rearrange("o (p a) -> p (o a)", a=PACK))
-        nc.sync.dma_start(g_rows[0][:], g_halves[0])
-        nc.sync.dma_start(g_list[:], offs2)
         with nc.allow_non_contiguous_dma(reason="one bound a partition and half"):
-            nc.sync.dma_start(cp_col[:, :, 0:1], cp.rearrange("(h p) o -> p h o", h=2))
+            nc.scalar.dma_start(cp_col[:, :, 0:1], cp.rearrange("(h p) o -> p h o", h=2))
+        nc.sync.dma_start(rb_col[:], rb.rearrange("o (p a) -> p (o a)", a=PACK))
+        nc.scalar.dma_start(ra_col[:], ra.rearrange("o (p a) -> p (o a)", a=PACK))
+        nc.sync.dma_start(g_rows[0][:], g_halves[0])
+        nc.scalar.dma_start(fk_col[:], fkr.rearrange("o (p a) -> p (o a)", a=PACK))
+        nc.sync.dma_start(g_list[:], offs2)
         nc.sync.dma_start(g_rows[1][:], g_halves[1])
-        nc.sync.dma_start(ra_col[:], ra.rearrange("o (p a) -> p (o a)", a=PACK))
-        nc.sync.dma_start(fk_col[:], fkr.rearrange("o (p a) -> p (o a)", a=PACK))
         nc.sync.dma_start(x_list[:], offs)
         nc.sync.dma_start(x_rows[0][:], x_planes[0])
         nc.sync.dma_start(x_rows[1][:], x_planes[1])

from contextlib import ExitStack

import concourse.mybir as mybir
from concourse.masks import make_identity

K, J, N, R, T, V = 512, 512, 256, 256, 1024, 1024
FLOPS = 2 * J * K * N + 2 * K * R * N

F32 = mybir.dt.float32
BF16 = mybir.dt.bfloat16
I32 = mybir.dt.int32
U32 = mybir.dt.uint32
U16 = mybir.dt.uint16
U8 = mybir.dt.uint8
E4M3 = mybir.dt.float8_e4m3fn_x4
E5M2 = mybir.dt.float8_e5m2_x4
ALU = mybir.AluOpType
COPY = mybir.ActivationFunctionType.Copy

P = 128
PACK = 4
KEEP = 0.05


def tile_list_directions_headpicks_bounded_larger_kernel(
    tc, xf, ra, gt, rb, cp, fkr, dr_words, dr_scales, old, offs, offs2, out
):
    nc = tc.nc
    with ExitStack() as ctx:
        lists = ctx.enter_context(tc.tile_pool(name="lists", bufs=1))
        held = ctx.enter_context(tc.tile_pool(name="held", bufs=1))
        psum = ctx.enter_context(tc.psum_pool(name="psum", bufs=1))
        turn = ctx.enter_context(tc.psum_pool(name="turn", bufs=4))

        x_list = lists.tile([P, J // 16], U16, name="x_list")
        g_list = lists.tile([P, J // 16], U16, name="g_list")
        x_rows = [held.tile([P, T], F32, name=f"x_rows{i}") for i in range(PACK)]
        g_rows = [held.tile([P, V], F32, name=f"g_rows{h}") for h in range(2)]
        ra_col = held.tile([P, PACK], F32, name="ra_col")
        rb_col = held.tile([P, PACK], F32, name="rb_col")
        fk_col = held.tile([P, PACK], F32, name="fk_col")
        cp_col = held.tile([P, 2, 8], F32, name="cp_col")
        dr_codes = held.tile([P, R], U32, name="dr_codes", align_bytes=64)
        dr_plane = held.tile([P, R], U8, name="dr_plane", align_bytes=64)
        old_rows = held.tile([P, 2, N], F32, name="old_rows")
        ident = held.tile([P, P], F32, name="ident")

        x_planes = xf.rearrange("(p i) t -> i p t", i=PACK)
        g_halves = gt.rearrange("(h p) v -> h p v", h=2)

        make_identity(nc, ident[:])
        nc.gpsimd.memset(dr_plane[:].bitcast(I32), 0)

        warm = held.tile([P, 2], F32, name="warm")
        nc.vector.memset(warm[:, 0:1], 0.0)
        nc.scalar.activation(warm[:, 1:2], warm[:, 0:1], COPY)
        with nc.allow_non_contiguous_dma(reason="one bound a partition and half"):
            nc.scalar.dma_start(cp_col[:, :, 0:1], cp.rearrange("(h p) o -> p h o", h=2))
        nc.sync.dma_start(rb_col[:], rb.rearrange("o (p a) -> p (o a)", a=PACK))
        nc.scalar.dma_start(ra_col[:], ra.rearrange("o (p a) -> p (o a)", a=PACK))
        nc.sync.dma_start(g_rows[0][:], g_halves[0])
        nc.scalar.dma_start(fk_col[:], fkr.rearrange("o (p a) -> p (o a)", a=PACK))
        nc.sync.dma_start(g_list[:], offs2)
        nc.sync.dma_start(g_rows[1][:], g_halves[1])
        nc.sync.dma_start(x_list[:], offs)
        nc.sync.dma_start(x_rows[0][:], x_planes[0])
        nc.sync.dma_start(x_rows[1][:], x_planes[1])
        nc.sync.dma_start(x_rows[2][:], x_planes[2])
        nc.sync.dma_start(x_rows[3][:], x_planes[3])
        nc.sync.dma_start(dr_codes[:].bitcast(I32), dr_words[0].rearrange("p n t -> p (n t)").bitcast(I32))
        for q in range(4):
            nc.sync.dma_start(
                dr_plane[32 * q : 32 * q + 4, :].bitcast(I32), dr_scales[0, 4 * q : 4 * q + 4, :].bitcast(I32)
            )
        nc.sync.dma_start(old_rows[:], old.rearrange("(h p) n -> p h n", h=2))

        def spread(col, name):
            bank = psum.tile([P, PACK, P], F32, name=name)
            for a in range(PACK):
                nc.tensor.transpose(bank[:, a, :], col[:, a : a + 1].to_broadcast([P, P]), ident[:])
            return bank[:].rearrange("p a m -> p m a")

        rb_all = spread(rb_col, "rb_all")
        ra_all = spread(ra_col, "ra_all")

        def on_scalar(picked, window):
            nc.scalar.activation(picked, window, COPY)

        on_vector = nc.vector.tensor_copy
        sources = [(g_rows[h], g_list, cp_col[:, h, 0:1], ALU.min, rb_all, E5M2) for h in range(2)]
        sources += [(x_rows[i], x_list, fk_col[:, i : i + 1], ALU.mult, ra_all, E4M3) for i in range(PACK)]
        shared = [[(0, 256, on_vector), (256, J, on_scalar)]]
        whole = [[(0, J, on_scalar)]]
        halves = [[(0, 256, on_scalar)], [(256, J, on_scalar)]]
        pieces = [shared, whole, shared, whole, whole, halves]

        def pick_weigh_turn(n):
            rows, offsets, scalar, op0, weights, fmt = sources[n]
            rounded = held.tile([P, J], BF16, name=f"rounded{n}", tag=f"rounded{n}", align_bytes=64)
            for m, gathers in enumerate(pieces[n]):
                first, last = gathers[0][0], gathers[-1][1]
                picked = held.tile([P, last - first], F32, name=f"picked{n}_{m}", tag=f"slot{n}_{m}", align_bytes=64)
                for a, b, gather in gathers:
                    gather(picked[:, a - first : b - first], rows[:].indirect(offsets[:, a // 16 : b // 16]))
                nc.vector.scalar_tensor_tensor(
                    rounded[:, first:last].rearrange("p (m a) -> p m a", a=PACK),
                    picked[:].rearrange("p (m a) -> p m a", a=PACK),
                    scalar,
                    weights[:, first // PACK : last // PACK, :],
                    op0,
                    ALU.mult,
                )
            words = rounded[:].bitcast(F32)
            turned = turn.tile([P, 2, P], F32, name="turned")
            for u in range(2):
                nc.tensor.transpose(turned[:, u, :], words[:, u::2], ident[:])
            return turned

        def quantise(n, turned, tag, empty):
            grouped = held.tile([P, J], BF16, name=f"grouped{n}", tag=tag, align_bytes=64)
            empty(
                grouped[:].bitcast(F32).rearrange("p (c u) -> p c u", u=2), turned[:].rearrange("p u c -> p c u")
            )
            codes = held.tile([P, P], U32, name=f"codes{n}", align_bytes=64)
            plane = held.tile([P, P], U8, name=f"plane{n}", align_bytes=64)
            nc.vector.quantize_mx(codes[:].bitcast(sources[n][5]), plane[:], grouped[:])
            return codes, plane

        w_banks = [psum.tile([P, PACK, P], F32, name=f"w_bank{h}") for h in range(2)]
        turned = [pick_weigh_turn(0), pick_weigh_turn(1)]
        operands = [quantise(0, turned[0], "grouped0", nc.vector.tensor_copy)]
        turned.append(pick_weigh_turn(2))
        operands.append(quantise(1, turned[1], "grouped1", nc.vector.tensor_copy))
        turned += [pick_weigh_turn(n) for n in range(3, 6)]
        for n, tag in zip(range(2, 6), ("slot4_0", "slot5_0", "slot5_1", "grouped5")):
            operands.append(quantise(n, turned[n], tag, nc.scalar.copy))
            for h in range(2):
                nc.tensor.matmul_mx(
                    w_banks[h][:, n - 2, :],
                    lhsT=operands[n][0][:].bitcast(E4M3),
                    lhsT_scale=operands[n][1][:],
                    rhs=operands[h][0][:].bitcast(E5M2),
                    rhs_scale=operands[h][1][:],
                    start=True,
                    stop=True,
                )
        old_kept = held.tile([P, 2, N], F32, name="old_kept", tag="rounded5", align_bytes=64)
        nc.scalar.mul(old_kept[:], old_rows[:], KEEP)

        w_ops = []
        w_grouped = [held.tile([P, K], BF16, name=f"w_grouped{h}", align_bytes=64) for h in range(2)]
        for h, evac in enumerate((nc.scalar.copy, nc.vector.tensor_copy)):
            evac(w_grouped[h][:].rearrange("p (n i) -> p n i", i=PACK), w_banks[h][:].rearrange("p i n -> p n i"))
        for h in range(2):
            w_codes = held.tile([P, P], U32, name=f"w_codes{h}", align_bytes=64)
            w_plane = held.tile([P, P], U8, name=f"w_plane{h}", align_bytes=64)
            nc.vector.quantize_mx(w_codes[:].bitcast(E5M2), w_plane[:], w_grouped[h][:])
            w_ops.append((w_codes, w_plane))
        out_halves = out.rearrange("(h p) n -> h p n", h=2)
        for rh in range(2):
            v2 = psum.tile([P, 2, P], F32, name=f"v2_{rh}", tag=("rb_all", "ra_all")[rh])
            for h in range(2):
                nc.tensor.matmul_mx(
                    v2[:, h, :],
                    lhsT=dr_codes[:, rh * P : (rh + 1) * P].bitcast(E4M3),
                    lhsT_scale=dr_plane[:, rh * P : (rh + 1) * P],
                    rhs=w_ops[h][0][:].bitcast(E5M2),
                    rhs_scale=w_ops[h][1][:],
                    start=True,
                    stop=True,
                )
            result = held.tile([P, N], F32, name=f"result{rh}")
            nc.vector.scalar_tensor_tensor(
                result[:], v2[:].rearrange("p h n -> p (h n)"), KEEP, old_kept[:, rh, :], ALU.mult, ALU.max
            )
            nc.sync.dma_start(out_halves[rh], result[:])
